import numpy as np
CORES = [9,41,49,65,73,81,97,113,15,47,55,71,79,87,103,119]
N = 16
def setup_inputs(rng):
    dy = rng.standard_normal((N, 128, N * 128), dtype=np.float32)
    dyt = np.concatenate([dy[:, :, 128 * j:128 * j + 128].transpose(0, 2, 1) for j in range(N)], axis=2)
    return {"x": rng.standard_normal((N, 128, 128), dtype=np.float32), "wt": rng.standard_normal((N, 128, 128), dtype=np.float32), "dy": dy, "dyt": dyt}
def setup_inputs_big(rng):
    d = setup_inputs(rng)
    for k in ("x", "wt", "dy", "dyt"): d[k] = (d[k].astype(np.float32) * 1024.0).astype(d[k].dtype)
    return d
def setup_inputs_small(rng):
    d = setup_inputs(rng)
    for k in ("x", "wt", "dy", "dyt"): d[k] = (d[k].astype(np.float32) * (1 / 1024.0)).astype(d[k].dtype)
    return d
def setup_inputs_apart(rng):
    d = setup_inputs(rng)
    f = (10.0 ** rng.permutation(np.linspace(-1.5, 1.5, N))).astype(np.float32).reshape(N, 1, 1)
    for k in ("x", "wt", "dy", "dyt"): d[k] = (d[k].astype(np.float32) * f).astype(d[k].dtype)
    return d
def tie_inputs(x):
    x = dict(x)
    x["dyt"] = np.concatenate([x["dy"][:, :, 128 * j:128 * j + 128].transpose(0, 2, 1) for j in range(N)], axis=2)
    return x
def reference(x, wt, dy, dyt):
    X, WT, DY, DYT = x.astype(np.float64), wt.astype(np.float64), dy.astype(np.float64), dyt.astype(np.float64)
    dx = np.zeros((N, 128, 128)); dw = np.zeros((N, 128, 128))
    for r in range(N):
        for j in range(N):
            dx[r] += WT[j].T @ DY[j][:, 128 * r:128 * r + 128]
            dw[r] += X[j].T @ DYT[r][:, 128 * j:128 * j + 128]
    return {"dx": dx.astype(np.float32 if x.dtype != np.float64 else np.float64), "dw": dw.astype(np.float32 if x.dtype != np.float64 else np.float64)}

from concourse.bass import DstId, RemoteDMATransfer
from concourse.mybir import AluOpType

B = 128
N = 16
NBANK = 7
NPIECE = 4

SCRATCH = {
    "xall": ("sbuf", [B, N * B], "float32"),
    "wts": ("sbuf", [B, B], "float32"),
    "dys": ("sbuf", [B, N * B], "float32"),
    "dts": ("sbuf", [B, N * B], "float32"),
    "P": ("sbuf", [B, N * B], "float32"),
    "pl": ("sbuf", [B, 8 * B], "float32"),
    "land": ("sbuf", [B, 7 * B], "float32"),
    "acc": ("sbuf", [B, B], "float32"),
    "dwb": ("sbuf", [B, B], "float32"),
    "xh": ("sbuf", [B, B], "float32"),
    "ha": ("sbuf", [B, 7 * B], "float32"),
    "hb": ("sbuf", [B, 7 * B], "float32"),
    "pw": ("psum", [B, 512], "float32"),
}
for _i in range(NBANK):
    SCRATCH["pp%d" % _i] = ("psum", [B, 512], "float32")

SEMAPHORES = (["sx", "swt", "gate", "va", "sdw", "vdw", "pls", "hx", "hp", "loc", "stx", "stw", "xf0", "xf1"]
              + ["sdy%d" % i for i in range(NPIECE)] + ["sdt%d" % i for i in range(NPIECE)]
              + ["pc%d" % i for i in range(NBANK)] + ["vc%d" % i for i in range(NBANK)]
              + ["xs%d" % i for i in range(8)] + ["ld%d" % i for i in range(8)])


def _bits(m):
    return [i for i in range(m.bit_length()) if (m >> i) & 1]


def _mk(lst):
    return sum(1 << i for i in lst)


def _cnt(m):
    return len(_bits(m))


def _plan(T, topo):
    cores = list(T.cores)
    chip, die = topo.chip, topo.die
    chips = sorted(set(chip(c) for c in cores))
    cidx = dict((ch, i) for i, ch in enumerate(chips))
    nch = len(chips)
    every = range(topo.CHIPS * topo.CORES_PER_CHIP)
    p = {"cores": cores, "cidx": cidx}
    partner, peers = {}, {}
    for R in cores:
        partner[R] = [r for r in cores if r != R and chip(r) == chip(R)][0]
        peers[R] = sorted([r for r in cores if chip(r) != chip(R) and die(r) == die(R)],
                          key=lambda r: (cidx[chip(r)] - cidx[chip(R)]) % nch)
    sender, D, src = {}, {}, {}
    for R in cores:
        helpers = [c for c in every if chip(c) == chip(R) and die(c) == die(R) and c not in cores]
        D[R] = []
        for h in helpers:
            D[h] = []
            src[h] = R
        for r in peers[R]:
            if topo.same_plane(chip(R), chip(r)):
                D[R].append(r)
                sender[(R, r)] = R
        for r in peers[R]:
            if (R, r) in sender:
                continue
            ok = [s for s in helpers + [R] if topo.may_write(s, r)]
            s = min(ok, key=lambda c: len(D[c]))
            D[s].append(r)
            sender[(R, r)] = s
    xdirect = dict((R, [r for r in peers[R] if topo.may_write(R, r)]) for R in cores)
    xrelay = dict((h, [r for r in D[h] if not topo.may_write(src[h], r)]) for h in src)
    xslot, lslot, bound, xorder, lorder = {}, {}, {}, {}, {}
    for r in cores:
        def xkey(R):
            if r in xdirect[R]:
                return (0, xdirect[R].index(r), cidx[chip(R)])
            return (1, xrelay[sender[(R, r)]].index(r), cidx[chip(R)])

        def lkey(R):
            s = sender[(R, r)]
            return (D[s].index(r), 0 if s == R else 1, cidx[chip(R)])
        xo = sorted(peers[r], key=xkey)
        lo = sorted(peers[r], key=lkey)
        xorder[r] = [r] + xo
        lorder[r] = lo
        for k, R in enumerate(xo):
            xslot[(r, R)] = 1 + k
        for k, R in enumerate(lo):
            lslot[(r, R)] = k
        nd = len([R for R in xo if r in xdirect[R]])
        bound[r] = 1 + nd if nd < len(xo) else (1 + len(xo)) // 2
    p.update(partner=partner, peers=peers, sender=sender, D=D, src=src, xdirect=xdirect, xrelay=xrelay,
             xslot=xslot, lslot=lslot, bound=bound, xorder=xorder, lorder=lorder)
    return p


def _blk(t, k, n=1):
    return t[:, k * B:(k + n) * B]


def _dst(topo, c):
    rid, pid, _s = topo.addr(c)
    return DstId(rid=rid, pnc=pid)


def _fold_send(g, T, topo, p, me, R, r, a, b):
    m = topo.mask(me, r)
    g.remote_dma_fused([RemoteDMATransfer(dst_ids=[_dst(topo, r)], dma_engine_mask=m,
                                          remote_sem=T.sem["ld%d" % p["cidx"][topo.chip(me)]],
                                          srcs=[a, b], dsts=[_blk(T.land, p["lslot"][(r, R)])], alu_op=1)],
                       local_sem=T.sem.loc)
    return _cnt(m)


def _helper(g, core, T, topo, p):
    R = p["src"][core]
    D = p["D"][core]
    loc = 0
    rel = p["xrelay"][core]
    if rel:
        g.wait_ge(T.sem.hx, _cnt(topo.mask(R, core)) // 2)
        m = topo.mask(core, rel[0])
        g.remote_dma_fused([RemoteDMATransfer(dst_ids=[_dst(topo, r) for r in rel], dma_engine_mask=m,
                                              remote_sem=T.sem["xs%d" % p["cidx"][topo.chip(core)]],
                                              srcs=[T.xh[:]], dsts=[_blk(T.xall, p["xslot"][(r, R)]) for r in rel])],
                           local_sem=T.sem.loc)
        loc += _cnt(m)
    g.wait_ge(T.sem.hp, _cnt(topo.mask(R, core)) + _cnt(topo.mask(p["partner"][R], core)))
    for i, r in enumerate(D):
        loc += _fold_send(g, T, topo, p, core, R, r, _blk(T.ha, i), _blk(T.hb, i))
    g.wait_ge(T.sem.loc, loc)


def rank_program(g, core, T, topo):
    p = _plan(T, topo)
    if T.rank_of(core) is None:
        if core in p["src"] and p["D"][core]:
            _helper(g, core, T, topo, p)
        return
    me = core
    cores, cidx, D = p["cores"], p["cidx"], p["D"]
    pa = p["partner"][me]
    rk = dict((c, i) for i, c in enumerate(cores))
    sem = T.sem
    pe, ve, sy, sc = g.tensor, g.vector, g.sync, g.scalar
    W = N * B // NPIECE

    sy.dma_start(_blk(T.xall, 0), T.x[:]).then_inc(sem.sx, 16)
    sc.dma_start(T.wts[:], T.wt[:]).then_inc(sem.swt, 16)
    for i in range(NPIECE):
        q = sc if i % 2 == 0 else sy
        q.dma_start(T.dys[:, i * W:(i + 1) * W], T.dy[:, i * W:(i + 1) * W]).then_inc(sem["sdy%d" % i], 16)
    sy.wait_ge(sem.gate, 1)
    sc.wait_ge(sem.gate, 1)
    for i in range(NPIECE):
        q = sc if i % 2 == 0 else sy
        q.dma_start(T.dts[:, i * W:(i + 1) * W], T.dyt[:, i * W:(i + 1) * W]).then_inc(sem["sdt%d" % i], 16)

    helpers = sorted([h for h in p["src"] if topo.chip(h) == topo.chip(me) and D[h]], key=lambda h: (-len(D[h]), h))
    groups = [(h, list(D[h])) for h in helpers] + [(pa, D[pa] + [pa]), (me, D[me] + [me])]
    chunks = []
    gchunks = []
    pos = 0
    for tgt, lst in groups:
        ids = []
        for a in range(0, len(lst), 4):
            ids.append(len(chunks))
            chunks.append((pos + a, lst[a:a + 4]))
        gchunks.append((tgt, pos, len(lst), ids))
        pos += len(lst)
    assert len(chunks) <= NBANK and pos == N

    pe.wait_ge(sem.swt, 16)
    seen = set()
    for ci, (p0, lst) in enumerate(chunks):
        for k, r in enumerate(lst):
            j = rk[r]
            if j * B // W not in seen:
                seen.add(j * B // W)
                pe.wait_ge(sem["sdy%d" % (j * B // W)], 16)
            pe.matmul(_blk(T["pp%d" % ci], k), T.wts[:], _blk(T.dys, j), True, True).then_inc(sem["pc%d" % ci], 1)
    b_me, b_pa = p["bound"][me], p["bound"][pa]
    nx = _cnt(topo.mask(me, p["peers"][me][0]))
    non = _cnt(topo.mask(pa, me))
    order = ([(k, p["xorder"][me][k], None) for k in range(0, b_me)]
             + [(8 + k, p["xorder"][pa][k], ("xf0", non)) for k in range(0, b_pa)]
             + [(k, p["xorder"][me][k], None) for k in range(b_me, 8)]
             + [(8 + k, p["xorder"][pa][k], ("xf1", non)) for k in range(b_pa, 8)])
    seen = set()
    waited = set()
    for n, (slot, R, w) in enumerate(order):
        j = rk[R]
        if j * B // W not in seen:
            seen.add(j * B // W)
            pe.wait_ge(sem["sdt%d" % (j * B // W)], 16)
        if w is None:
            w = ("sx", 16) if R == me else ("xs%d" % cidx[topo.chip(R)], nx)
        if w[0] not in waited:
            waited.add(w[0])
            pe.wait_ge(sem[w[0]], w[1])
        pe.matmul(T.pw[:, 0:B], _blk(T.xall, slot), _blk(T.dts, j), n == 0, n == len(order) - 1).then_inc(sem.sdw, 1)

    for ci, (p0, lst) in enumerate(chunks):
        ve.wait_ge(sem["pc%d" % ci], len(lst))
        ve.tensor_copy(_blk(T.P, p0, len(lst)), T["pp%d" % ci][:, 0:len(lst) * B]).then_inc(sem["vc%d" % ci], 1)
    ve.wait_ge(sem["vc%d" % (len(chunks) - 1)], 1)
    ve.wait_ge(sem.pls, non)
    ve.tensor_tensor(T.acc[:], _blk(T.P, N - 1), _blk(T.pl, len(D[me])), AluOpType.add).then_inc(sem.va, 1)
    na = 1
    for k, R in enumerate(p["lorder"][me]):
        ve.wait_ge(sem["ld%d" % cidx[topo.chip(R)]], nx)
        ve.wait_ge(sem.va, na)
        ve.tensor_tensor(T.acc[:], T.acc[:], _blk(T.land, k), AluOpType.add).then_inc(sem.va, 1)
        na += 1
    ve.wait_ge(sem.sdw, len(order))
    ve.tensor_copy(T.dwb[:], T.pw[:, 0:B]).then_inc(sem.vdw, 1)

    sy.wait_ge(sem.va, na)
    sy.dma_start(T.dx[:], T.acc[:]).then_inc(sem.stx, 16)
    sc.wait_ge(sem.vdw, 1)
    sc.dma_start(T.dw[:], T.dwb[:]).then_inc(sem.stw, 16)

    loc = 0
    g.wait_ge(sem.sx, 16)
    xd = p["xdirect"][me]
    moff = topo.mask(me, xd[0])
    tr = [RemoteDMATransfer(dst_ids=[_dst(topo, r) for r in xd], dma_engine_mask=moff,
                            remote_sem=sem["xs%d" % cidx[topo.chip(me)]], srcs=[_blk(T.xall, 0)],
                            dsts=[_blk(T.xall, p["xslot"][(r, me)]) for r in xd])]
    loc += _cnt(moff)
    rel = [h for h in helpers if p["src"][h] == me and p["xrelay"][h]]
    if rel:
        rest = [e for e in _bits(topo.mask(me, rel[0])) if e not in _bits(moff)]
        mon = _mk(rest)
        assert _cnt(mon) * 2 == _cnt(topo.mask(me, rel[0]))
        tr.append(RemoteDMATransfer(dst_ids=[_dst(topo, h) for h in rel], dma_engine_mask=mon, remote_sem=sem.hx,
                                    srcs=[_blk(T.xall, 0)], dsts=[T.xh[:] for h in rel]))
        loc += _cnt(mon)
    g.remote_dma_fused(tr, local_sem=sem.loc)
    g.sem_inc(sem.gate, 1)

    for tgt, p0, w, ids in gchunks[:-1]:
        for ci in ids:
            g.wait_ge(sem["vc%d" % ci], 1)
        rid, pid, _s = topo.addr(tgt)
        m = topo.mask(me, tgt)
        if tgt == pa:
            out, rs = T.pl[:, 0:w * B], sem.pls
        else:
            out, rs = (T.ha if p["src"][tgt] == me else T.hb)[:, 0:w * B], sem.hp
        g.remote_dma(out, _blk(T.P, p0, w), rs, sem.loc, pid, rid, m)
        loc += _cnt(m)

    _t, p0, w, ids = gchunks[-1]
    for ci in ids:
        g.wait_ge(sem["vc%d" % ci], 1)
    g.wait_ge(sem.pls, non)
    for i, r in enumerate(D[me]):
        loc += _fold_send(g, T, topo, p, me, me, r, _blk(T.P, p0 + i), _blk(T.pl, i))

    rid, pid, _s = topo.addr(pa)
    m = topo.mask(me, pa)
    for name, lo, hi in (("xf0", 0, b_me), ("xf1", b_me, 8)):
        for k in range(max(lo, 1), hi):
            g.wait_ge(sem["xs%d" % cidx[topo.chip(p["xorder"][me][k])]], nx)
        g.remote_dma(_blk(T.xall, 8 + lo, hi - lo), _blk(T.xall, lo, hi - lo), sem[name], sem.loc, pid, rid, m)
        loc += _cnt(m)

    g.wait_ge(sem.loc, loc)
    g.wait_ge(sem.stx, 16)
    g.wait_ge(sem.stw, 16)
